import numpy as np
import ml_dtypes


def mxq(x, axis, fmt="e4m3"):
    dtype, down = {"e4m3": (ml_dtypes.float8_e4m3fn, 7), "e5m2": (ml_dtypes.float8_e5m2, 14)}[fmt]
    v = np.moveaxis(np.asarray(x, np.float32).astype(ml_dtypes.bfloat16).astype(np.float64), axis, -1)
    blocks = v.reshape(v.shape[:-1] + (-1, 32))
    amax = np.abs(blocks).max(-1, keepdims=True)
    byte = np.maximum(np.where(amax > 0, np.frexp(amax)[1] - 1 + 127, 0) - down, 1)
    scale = np.exp2(byte - 127.0)
    codes = (blocks / scale).astype(np.float32).astype(dtype).astype(np.float64)
    return np.moveaxis((codes * scale).reshape(v.shape), -1, axis)


WIDE = False


def mx_kscale(k):
    if not WIDE:
        return np.ones(k)
    levels = np.array([10, -10, 5, -5, 0])
    if k % 512:
        return np.exp2(np.random.permutation(np.resize(levels, k // 32))).repeat(32)
    a = np.empty((k // 512, 16))
    for p in range(k // 512):
        a[p, :8] = np.random.permutation(np.resize(levels, 8))
        for g in range(8):
            far = levels[np.abs(levels - a[p, g]) >= 10]
            a[p, g + 8] = far[np.random.randint(len(far))]
    return np.exp2(a.ravel()).repeat(32)


def f64(x):
    return np.asarray(x).astype(np.float64)


def striped(idx):
    return np.tile(idx.reshape(-1, 16).T, (8, 1)).astype(np.uint16)


def unstriped(offs):
    return offs[:16].T.reshape(-1).astype(np.int64)


def striped8(idx):
    return np.concatenate([x.reshape(-1, 16).T for x in idx]).astype(np.uint16)


def runs(offs, k):
    lists = np.stack([offs[16 * r : 16 * r + 16].T.reshape(-1) for r in range(8)]).astype(np.int64)
    return lists[np.arange(k) % 512 // 64]


def pack_weight(w):
    k, n = w.shape
    w = f64(np.asarray(w, np.float32).astype(ml_dtypes.bfloat16)).reshape(k // 32, 32, n)
    amax = np.abs(w).max(1)
    byte = np.clip(np.where(amax > 0, np.frexp(amax)[1] - 1 + 127 - 7, 1), 1, 254)
    scaled = (w * np.exp2(127.0 - byte)[:, None, :]).reshape(k, n).astype(np.float32)
    words = np.ascontiguousarray(scaled.reshape(k // 512, 128, 4, n).transpose(0, 1, 3, 2)).astype(ml_dtypes.float8_e4m3fn).view(np.uint8)
    return words, np.ascontiguousarray(byte.astype(np.uint8).reshape(k // 512, 16, n))


def unpack_weight(words, scales):
    g, p, n, _ = words.shape
    vals = np.ascontiguousarray(words).view(ml_dtypes.float8_e4m3fn).astype(np.float64) * np.repeat(np.exp2(scales.astype(np.float64) - 127.0), 8, axis=1)[..., None]
    return vals.transpose(0, 1, 3, 2).reshape(g * 512, n)


K, T, S, H, W, C, U = 512, 2048, 256, 512, 128, 512, 512


def setup_inputs():
    n = np.random.standard_normal
    s = mx_kscale(K)[:, None]
    packed_xT = pack_weight(n((K, T)) * s)
    perm = np.random.permutation(S)
    perm2 = np.random.permutation(S)
    perm3 = np.random.permutation(U)
    return {
        "x_words": packed_xT[0],
        "x_scales": packed_xT[1],
        "w1": (n((K, H)) / np.sqrt(2 * K) / s).astype(np.float32),
        "w2": (n((K, H)) / np.sqrt(2 * K) / s).astype(np.float32),
        "gs": (np.random.uniform(0.5, 1.5, (K, 1)) / s).astype(np.float32),
        "offs": striped(np.random.permutation(T)[:S]),
        "two": striped(np.random.permutation(T)[:S]),
        "n1": striped(perm[:W]),
        "n2": striped(perm[W:]),
        "n3": striped(perm2[:W]),
        "n4": striped(perm2[W:]),
        "cand": striped8(np.random.randint(0, T, (8, C))),
        "n5": striped(perm3[:S]),
        "n6": striped(perm3[S:]),
        "n7": striped(np.random.permutation(S)),
        "n8": striped(np.random.permutation(S)),
    }


def reference(x_words, x_scales, w1, w2, gs, offs, two, n1, n2, n3, n4, cand, n5, n6, n7, n8):
    x_cand = unpack_weight(x_words, x_scales)[np.arange(K)[:, None], runs(cand, K)]
    xq = unpack_weight(x_words, x_scales)[:, unstriped(offs)]
    x_two = unpack_weight(x_words, x_scales)[:, unstriped(two)]
    y = mxq(f64(w1), 0, "e4m3").T @ xq + mxq(f64(w2), 0, "e4m3").T @ x_two
    pa = y[:, unstriped(n1)]
    pb = y[:, unstriped(n2)]
    rb = pa - pb
    ra = np.maximum(pa, pb)
    ua = np.zeros((H, S))
    ua[:, unstriped(n3)] = ra
    ub = ua.copy()
    ub[:, unstriped(n4)] = rb
    z = f64(gs) * ub
    s = 0.0625 * ((x_cand.T @ mxq(z, 0, "e4m3")))
    st = s - s[:, unstriped(n7)]
    up = np.maximum(st, st[:, unstriped(n8)])
    ph = np.zeros((C, U))
    ph[:, unstriped(n5)] = st
    out = ph.copy()
    out[:, unstriped(n6)] = up
    return out

@@ -1,0 +1,260 @@
+from contextlib import ExitStack
+
+import concourse.mybir as mybir
+
+F32 = mybir.dt.float32
+BF16 = mybir.dt.bfloat16
+I32 = mybir.dt.int32
+U32 = mybir.dt.uint32
+U16 = mybir.dt.uint16
+U8 = mybir.dt.uint8
+FP8X4 = mybir.dt.float8_e4m3fn_x4
+COPY = mybir.ActivationFunctionType.Copy
+MULT = mybir.AluOpType.mult
+MAX = mybir.AluOpType.max
+SUB = mybir.AluOpType.subtract
+
+P = 128
+HALF = 64
+PACK = 4
+T = 2048
+S = 256
+W = 128
+C = 512
+U = 512
+PER_COL = 16
+SCORE_SCALE = 0.0625
+
+FLOPS = 402653184
+
+
+def tile_picked_dttzkcpmxpagew_none_p_kernel(
+    tc, x_words, x_scales, w1, w2, gs, offs, two, n1, n2, n3, n4, cand, n5, n6, n7, n8, out
+):
+    nc = tc.nc
+    with ExitStack() as ctx:
+        keep = ctx.enter_context(tc.tile_pool(name="keep", bufs=1))
+        psum = ctx.enter_context(tc.psum_pool(name="psum", bufs=1))
+
+        def load_list(src, name):
+            lst = keep.tile(list(src.shape), U16, name=name)
+            nc.sync.dma_start(lst[:], src)
+            return lst
+
+        def load_w(w, half, name):
+            raw = keep.tile([P, PACK, 2 * P], F32, name=name)
+            cols = slice(2 * P * half, 2 * P * (half + 1))
+            nc.sync.dma_start(raw[:], w.rearrange("(p j) c -> p j c", j=PACK)[:, :, cols])
+            return raw
+
+        xs = keep.tile([P, T], U8, name="xs", align_bytes=64)
+        nc.vector.memset(xs[:].bitcast(I32), 0)
+        offs_t = load_list(offs, "offs_t")
+        w_lo = [load_w(w1, 0, "w1_lo")]
+        two_t = load_list(two, "two_t")
+        for r, part_step in ((0, 16), (1, 16), (2, 32), (3, 32)):
+            nc.sync.dma_start(
+                xs[r:P:part_step, :].bitcast(I32), x_scales[0, r : 16 : part_step // 8, :].bitcast(I32)
+            )
+        xw = keep.tile([P, T], U32, name="xw", align_bytes=64)
+        nc.sync.dma_start(xw[:].bitcast(I32), x_words[0].rearrange("p n t -> p (n t)").bitcast(I32))
+        w_lo.append(load_w(w2, 0, "w2_lo"))
+        n1_t = load_list(n1, "n1_t")
+        n2_t = load_list(n2, "n2_t")
+        w_hi = [load_w(w1, 1, "w1_hi")]
+        n3_t = load_list(n3, "n3_t")
+        n4_t = load_list(n4, "n4_t")
+        w_hi.append(load_w(w2, 1, "w2_hi"))
+        cand_t = load_list(cand, "cand_t")
+        gs_t = keep.tile([P, PACK], F32, name="gs_t")
+        nc.sync.dma_start(gs_t[:], gs.rearrange("(p t) o -> p (t o)", t=PACK))
+        n7_t = load_list(n7, "n7_t")
+        n8_t = load_list(n8, "n8_t")
+        n5_t = load_list(n5, "n5_t")
+        n6_t = load_list(n6, "n6_t")
+
+        def gather_packed(window, lst, first, n, dtype, name, tag):
+            got = keep.tile([P, n], dtype, name=name, tag=tag, align_bytes=64)
+            for c0 in range(0, n, S):
+                nc.vector.tensor_copy(
+                    got[:, c0 : c0 + S],
+                    window[:].indirect(lst[:, (first + c0) // PER_COL : (first + c0 + S) // PER_COL]),
+                )
+            return got
+
+        tok_scales = [
+            gather_packed(xs, offs_t, 0, S, U8, "offs_s", "offs_s"),
+            gather_packed(xs, two_t, 0, S, U8, "two_s", "two_s"),
+        ]
+        tok_words = [
+            gather_packed(xw, offs_t, 0, S, U32, "offs_w", "offs_w"),
+            gather_packed(xw, two_t, 0, S, U32, "two_w", "two_w"),
+        ]
+
+        staged = [
+            [keep.tile([P, n * P, PACK], BF16, name="stg%d_%d" % (i, g), align_bytes=64) for g, n in enumerate((1, 1, 2))]
+            for i in range(2)
+        ]
+        w_codes = [
+            [keep.tile([P, n * P], U32, name="wc%d_%d" % (i, g), align_bytes=64) for g, n in enumerate((1, 1, 2))]
+            for i in range(2)
+        ]
+        w_scales = [
+            [keep.tile([P, n * P], U8, name="ws%d_%d" % (i, g), align_bytes=64) for g, n in enumerate((1, 1, 2))]
+            for i in range(2)
+        ]
+
+        def by_class(raw):
+            return raw[:].rearrange("p j (m e) -> p m j e", e=PACK)
+
+        def cast_01(copy, i, half, raw):
+            copy(staged[i][half][:].rearrange("p (e m) j -> p m j e", e=2), by_class(raw)[:, :, :, 0:2])
+
+        def cast_23(copy, i, half, raw):
+            dst = staged[i][2][:].rearrange("p (e m) j -> p m j e", e=2)
+            copy(dst[:, HALF * half : HALF * (half + 1), :, :], by_class(raw)[:, :, :, 2:4])
+
+        def quantize_w(i, g):
+            nc.vector.quantize_mx(
+                out=w_codes[i][g][:].bitcast(FP8X4),
+                scales=w_scales[i][g][:],
+                in_=staged[i][g][:].rearrange("p m j -> p (m j)"),
+            )
+
+        y_ps = [psum.tile([P, S], F32, name="y_ps%d" % t) for t in range(PACK)]
+        y_sb = [keep.tile([P, S], F32, name="y_sb%d" % t, align_bytes=64) for t in range(PACK)]
+        pa = [keep.tile([P, W], F32, name="pa%d" % t, align_bytes=64) for t in range(PACK)]
+        pb = [keep.tile([P, W], F32, name="pb%d" % t) for t in range(PACK)]
+        ra = [keep.tile([P, W], F32, name="ra%d" % t) for t in range(PACK)]
+        rb = [keep.tile([P, W], F32, name="rb%d" % t) for t in range(PACK)]
+        ub = [keep.tile([P, S], F32, name="ub%d" % t) for t in range(PACK)]
+        dealt = [keep.tile([P, S], F32, name="dealt%d" % e) for e in range(2)]
+        z_bf = keep.tile([P, S, PACK], BF16, name="z_bf", align_bytes=64)
+
+        def product_y(t):
+            g = min(t, 2)
+            cols = slice(P * (t - g), P * (t - g + 1))
+            for i in range(2):
+                nc.tensor.matmul_mx(
+                    out=y_ps[t][:],
+                    lhsT=w_codes[i][g][:, cols].bitcast(FP8X4),
+                    lhsT_scale=w_scales[i][g][:, cols],
+                    rhs=tok_words[i][:].bitcast(FP8X4),
+                    rhs_scale=tok_scales[i][:],
+                    start=(i == 0),
+                    stop=(i == 1),
+                )
+
+        def fetch_pairs(t):
+            nc.scalar.activation(pa[t][:], y_sb[t][:].indirect(n1_t[:]), COPY)
+            nc.scalar.activation(pb[t][:], y_sb[t][:].indirect(n2_t[:]), COPY)
+
+        def combine_pairs(t):
+            nc.vector.tensor_tensor(ra[t][:], pa[t][:], pb[t][:], MAX)
+            nc.vector.tensor_tensor(rb[t][:], pa[t][:], pb[t][:], SUB)
+
+        def put_pairs(t):
+            nc.scalar.activation(ub[t][:].indirect(n3_t[:]), ra[t][:], COPY)
+            nc.scalar.activation(ub[t][:].indirect(n4_t[:]), rb[t][:], COPY)
+
+        def deal(t):
+            for e in range(2):
+                nc.sync.dma_start(dealt[e][HALF * t : HALF * (t + 1), :], ub[t][HALF * e : HALF * (e + 1), :])
+
+        def weigh(src, e):
+            nc.vector.tensor_scalar(z_bf[:, :, e], src[:], gs_t[:, e : e + 1], None, MULT)
+
+        cast_01(nc.scalar.copy, 0, 0, w_lo[0])
+        cast_23(nc.scalar.copy, 0, 0, w_lo[0])
+        quantize_w(0, 0)
+        cast_01(nc.vector.tensor_copy, 1, 0, w_lo[1])
+        cast_23(nc.scalar.copy, 1, 0, w_lo[1])
+        quantize_w(1, 0)
+        product_y(0)
+        nc.scalar.copy(y_sb[0][:], y_ps[0][:])
+        fetch_pairs(0)
+        combine_pairs(0)
+        put_pairs(0)
+        deal(0)
+        cast_01(nc.vector.tensor_copy, 0, 1, w_hi[0])
+        quantize_w(0, 1)
+        cast_01(nc.vector.tensor_copy, 1, 1, w_hi[1])
+        quantize_w(1, 1)
+        product_y(1)
+        nc.vector.tensor_copy(y_sb[1][:], y_ps[1][:])
+        fetch_pairs(1)
+        combine_pairs(1)
+        put_pairs(1)
+        deal(1)
+        for i in range(2):
+            cast_23(nc.vector.tensor_copy, i, 1, w_hi[i])
+            quantize_w(i, 2)
+        for t in (2, 3):
+            product_y(t)
+            nc.vector.tensor_copy(y_sb[t][:], y_ps[t][:])
+        cand_bytes = gather_packed(xs, cand_t, 0, C, U8, "cand_bytes", "pa1")
+        cand_scales = keep.tile([P, C], U8, name="cand_scales", align_bytes=64)
+        nc.vector.memset(cand_scales[:].bitcast(I32), 0)
+        for r, first in ((0, 0), (1, 1), (2, 16), (3, 17)):
+            nc.sync.dma_start(cand_scales[r:P:32, :].bitcast(I32), cand_bytes[first:P:32, :].bitcast(I32))
+        for t in (2, 3):
+            fetch_pairs(t)
+            combine_pairs(t)
+        cand_words = [gather_packed(xw, cand_t, S * h, S, U32, "cand_words%d" % h, "y_sb%d" % (2 + h)) for h in range(2)]
+        put_pairs(2)
+        put_pairs(3)
+        weigh(dealt[0], 0)
+        weigh(dealt[1], 1)
+        weigh(ub[2], 2)
+        weigh(ub[3], 3)
+
+        z_codes = keep.tile([P, S], U32, name="z_codes", align_bytes=64)
+        z_scales = keep.tile([P, S], U8, name="z_scales", align_bytes=64)
+        nc.vector.quantize_mx(
+            out=z_codes[:].bitcast(FP8X4), scales=z_scales[:], in_=z_bf[:].rearrange("p s t -> p (s t)")
+        )
+
+        blocks = C // P
+        s_ps = [psum.tile([P, S], F32, name="s_ps%d" % b) for b in range(blocks)]
+        s_sb = [keep.tile([P, S], F32, name="s_sb%d" % b) for b in range(blocks)]
+        s_n7 = [keep.tile([P, S], F32, name="s_n7_%d" % b) for b in range(blocks)]
+        st = [keep.tile([P, S], F32, name="st%d" % b) for b in range(blocks)]
+        st_n8 = [keep.tile([P, S], F32, name="st_n8_%d" % b) for b in range(blocks)]
+        up = [keep.tile([P, S], F32, name="up%d" % b) for b in range(blocks)]
+        page = [keep.tile([P, U], F32, name="page%d" % b) for b in range(blocks)]
+
+        def fetch_halves(dst, window, lst):
+            for c0 in range(0, S, W):
+                nc.scalar.activation(
+                    dst[:, c0 : c0 + W], window[:].indirect(lst[:, c0 // PER_COL : (c0 + W) // PER_COL]), COPY
+                )
+
+        for b in range(blocks):
+            cols = slice(P * b, P * (b + 1))
+            nc.tensor.matmul_mx(
+                out=s_ps[b][:],
+                lhsT=cand_words[b // 2][:, P * (b % 2) : P * (b % 2 + 1)].bitcast(FP8X4),
+                lhsT_scale=cand_scales[:, cols],
+                rhs=z_codes[:].bitcast(FP8X4),
+                rhs_scale=z_scales[:],
+                start=True,
+                stop=True,
+            )
+            if b == 0:
+                nc.scalar.activation(s_sb[b][:], s_ps[b][:], COPY, scale=SCORE_SCALE)
+            else:
+                nc.vector.tensor_scalar(s_sb[b][:], s_ps[b][:], SCORE_SCALE, None, MULT)
+
+        def first_step(b):
+            fetch_halves(s_n7[b], s_sb[b], n7_t)
+            nc.vector.tensor_tensor(st[b][:], s_sb[b][:], s_n7[b][:], SUB)
+
+        first_step(0)
+        for b in range(blocks):
+            if b + 1 < blocks:
+                first_step(b + 1)
+            fetch_halves(st_n8[b], st[b], n8_t)
+            nc.vector.tensor_tensor(up[b][:], st[b][:], st_n8[b][:], MAX)
+            nc.scalar.activation(page[b][:].indirect(n5_t[:]), st[b][:], COPY)
+            nc.scalar.activation(page[b][:].indirect(n6_t[:]), up[b][:], COPY)
+            nc.sync.dma_start(out[P * b : P * (b + 1), :], page[b][:])

@@ -73,151 +73,147 @@ def tile_picked_dttzkcpmxpagew_none_p_kernel(
         n5_t = load_list(n5, "n5_t")
         n6_t = load_list(n6, "n6_t")
 
-        def gather_packed(window, lst, first, n, dtype, name, tag):
-            got = keep.tile([P, n], dtype, name=name, tag=tag, align_bytes=64)
-            for c0 in range(0, n, S):
-                nc.vector.tensor_copy(
-                    got[:, c0 : c0 + S],
-                    window[:].indirect(lst[:, (first + c0) // PER_COL : (first + c0 + S) // PER_COL]),
-                )
+        def gather_packed(window, lst, first, dtype, name, tag):
+            got = keep.tile([P, S], dtype, name=name, tag=tag, align_bytes=64)
+            nc.vector.tensor_copy(got[:], window[:].indirect(lst[:, first // PER_COL : (first + S) // PER_COL]))
             return got
 
-        tok_scales = [
-            gather_packed(xs, offs_t, 0, S, U8, "offs_s", "offs_s"),
-            gather_packed(xs, two_t, 0, S, U8, "two_s", "two_s"),
-        ]
-        tok_words = [
-            gather_packed(xw, offs_t, 0, S, U32, "offs_w", "offs_w"),
-            gather_packed(xw, two_t, 0, S, U32, "two_w", "two_w"),
-        ]
+        def candidate_scales(h, tag):
+            picked = gather_packed(xs, cand_t, S * h, U8, "cand_bytes%d" % h, tag)
+            placed = keep.tile([P, S], U8, name="cand_scales%d" % h, align_bytes=64)
+            nc.vector.tensor_copy(placed[:].bitcast(I32), picked[:].bitcast(I32))
+            for r in (2, 3):
+                nc.sync.dma_start(placed[r:P:32, :].bitcast(I32), picked[14 + r : P : 32, :].bitcast(I32))
+            return placed
 
-        staged = [
-            [keep.tile([P, n * P, PACK], BF16, name="stg%d_%d" % (i, g), align_bytes=64) for g, n in enumerate((1, 1, 2))]
+        tok_scales = [gather_packed(xs, offs_t, 0, U8, "offs_s", "offs_s"), gather_packed(xs, two_t, 0, U8, "two_s", "two_s")]
+        tok_words = [gather_packed(xw, offs_t, 0, U32, "offs_w", "offs_w"), gather_packed(xw, two_t, 0, U32, "two_w", "two_w")]
+
+        w_scales = {
+            (i, t): keep.tile([P, P], U8, name="ws%d_%d" % (i, t), align_bytes=64) for i in range(2) for t in range(PACK)
+        }
+        w_codes = {
+            (i, t): keep.tile([P, P], U32, name="wc%d_%d" % (i, t), align_bytes=64)[:]
             for i in range(2)
-        ]
-        w_codes = [
-            [keep.tile([P, n * P], U32, name="wc%d_%d" % (i, g), align_bytes=64) for g, n in enumerate((1, 1, 2))]
-            for i in range(2)
-        ]
-        w_scales = [
-            [keep.tile([P, n * P], U8, name="ws%d_%d" % (i, g), align_bytes=64) for g, n in enumerate((1, 1, 2))]
-            for i in range(2)
-        ]
+            for t in range(2)
+        }
 
-        def by_class(raw):
-            return raw[:].rearrange("p j (m e) -> p m j e", e=PACK)
+        def cast(copy, dst, raw, first_class, ms):
+            src = raw[:].rearrange("p j (m e) -> p m e j", e=PACK)
+            copy(dst.rearrange("p e m j -> p m e j")[:, ms, :, :], src[:, ms, first_class : first_class + 2, :])
 
-        def cast_01(copy, i, half, raw):
-            copy(staged[i][half][:].rearrange("p (e m) j -> p m j e", e=2), by_class(raw)[:, :, :, 0:2])
-
-        def cast_23(copy, i, half, raw):
-            dst = staged[i][2][:].rearrange("p (e m) j -> p m j e", e=2)
-            copy(dst[:, HALF * half : HALF * (half + 1), :, :], by_class(raw)[:, :, :, 2:4])
-
-        def quantize_w(i, g):
-            nc.vector.quantize_mx(
-                out=w_codes[i][g][:].bitcast(FP8X4),
-                scales=w_scales[i][g][:],
-                in_=staged[i][g][:].rearrange("p m j -> p (m j)"),
-            )
+        def quantize_w(i, t, staged):
+            nc.vector.quantize_mx(out=w_codes[i, t].bitcast(FP8X4), scales=w_scales[i, t][:], in_=staged)
 
         y_ps = [psum.tile([P, S], F32, name="y_ps%d" % t) for t in range(PACK)]
         y_sb = [keep.tile([P, S], F32, name="y_sb%d" % t, align_bytes=64) for t in range(PACK)]
-        pa = [keep.tile([P, W], F32, name="pa%d" % t, align_bytes=64) for t in range(PACK)]
-        pb = [keep.tile([P, W], F32, name="pb%d" % t) for t in range(PACK)]
-        ra = [keep.tile([P, W], F32, name="ra%d" % t) for t in range(PACK)]
-        rb = [keep.tile([P, W], F32, name="rb%d" % t) for t in range(PACK)]
-        ub = [keep.tile([P, S], F32, name="ub%d" % t) for t in range(PACK)]
-        dealt = [keep.tile([P, S], F32, name="dealt%d" % e) for e in range(2)]
-        z_bf = keep.tile([P, S, PACK], BF16, name="z_bf", align_bytes=64)
+        pa, pb, ra = {}, {}, {}
+        ub = [keep.tile([P, S], F32, name="ub%d" % t, align_bytes=64) for t in range(PACK)]
+        dealt = [keep.tile([P, S], F32, name="dealt%d" % e, align_bytes=64) for e in range(2)]
 
         def product_y(t):
-            g = min(t, 2)
-            cols = slice(P * (t - g), P * (t - g + 1))
             for i in range(2):
                 nc.tensor.matmul_mx(
                     out=y_ps[t][:],
-                    lhsT=w_codes[i][g][:, cols].bitcast(FP8X4),
-                    lhsT_scale=w_scales[i][g][:, cols],
+                    lhsT=w_codes[i, t].bitcast(FP8X4),
+                    lhsT_scale=w_scales[i, t][:],
                     rhs=tok_words[i][:].bitcast(FP8X4),
                     rhs_scale=tok_scales[i][:],
                     start=(i == 0),
                     stop=(i == 1),
                 )
 
-        def fetch_pairs(t):
-            nc.scalar.activation(pa[t][:], y_sb[t][:].indirect(n1_t[:]), COPY)
-            nc.scalar.activation(pb[t][:], y_sb[t][:].indirect(n2_t[:]), COPY)
+        def pair_tile(name, t, tag):
+            return keep.tile([P, W], F32, name="%s%d" % (name, t), tag=tag, align_bytes=64)
 
-        def combine_pairs(t):
-            nc.vector.tensor_tensor(ra[t][:], pa[t][:], pb[t][:], MAX)
-            nc.vector.tensor_tensor(rb[t][:], pa[t][:], pb[t][:], SUB)
+        def fetch_pairs(t, dst_a, dst_b):
+            pa[t], pb[t] = dst_a, dst_b
+            nc.scalar.activation(pa[t], y_sb[t][:].indirect(n1_t[:]), COPY)
+            nc.scalar.activation(pb[t], y_sb[t][:].indirect(n2_t[:]), COPY)
 
-        def put_pairs(t):
+        def put_larger(t, tag):
+            ra[t] = pair_tile("ra", t, tag)
+            nc.vector.tensor_tensor(ra[t][:], pa[t], pb[t], MAX)
             nc.scalar.activation(ub[t][:].indirect(n3_t[:]), ra[t][:], COPY)
-            nc.scalar.activation(ub[t][:].indirect(n4_t[:]), rb[t][:], COPY)
+
+        def put_difference(t, tag):
+            rb = pair_tile("rb", t, tag)
+            nc.vector.tensor_tensor(rb[:], pa[t], pb[t], SUB)
+            nc.scalar.activation(ub[t][:].indirect(n4_t[:]), rb[:], COPY)
 
         def deal(t):
             for e in range(2):
                 nc.sync.dma_start(dealt[e][HALF * t : HALF * (t + 1), :], ub[t][HALF * e : HALF * (e + 1), :])
 
-        def weigh(src, e):
-            nc.vector.tensor_scalar(z_bf[:, :, e], src[:], gs_t[:, e : e + 1], None, MULT)
+        def weigh(src, e, cols):
+            nc.vector.tensor_scalar(z_bf[:, cols, e], src[:, cols], gs_t[:, e : e + 1], None, MULT)
 
-        cast_01(nc.scalar.copy, 0, 0, w_lo[0])
-        cast_23(nc.scalar.copy, 0, 0, w_lo[0])
-        quantize_w(0, 0)
-        cast_01(nc.vector.tensor_copy, 1, 0, w_lo[1])
-        cast_23(nc.scalar.copy, 1, 0, w_lo[1])
-        quantize_w(1, 0)
+        quarter = HALF // 2
+        whole = slice(0, HALF)
+        lo01 = [keep.tile([P, 2, HALF, PACK], BF16, name="lo01_%d" % i, align_bytes=64) for i in range(2)]
+        hi01 = [keep.tile([P, 2, HALF, PACK], BF16, name="hi01_%d" % i, align_bytes=64) for i in range(2)]
+        all23 = [keep.tile([P, 2, P, PACK], BF16, name="all23_%d" % i, align_bytes=64) for i in range(2)]
+        cast(nc.scalar.copy, lo01[0][:], w_lo[0], 0, whole)
+        cast(nc.scalar.copy, all23[0][:, :, 0:HALF, :], w_lo[0], 2, whole)
+        quantize_w(0, 0, lo01[0][:].rearrange("p e m j -> p (e m j)"))
+        cast(nc.vector.tensor_copy, lo01[1][:], w_lo[1], 0, slice(0, quarter))
+        cast(nc.scalar.copy, lo01[1][:], w_lo[1], 0, slice(quarter, HALF))
+        quantize_w(1, 0, lo01[1][:].rearrange("p e m j -> p (e m j)"))
+        cast(nc.scalar.copy, all23[1][:, :, 0:HALF, :], w_lo[1], 2, whole)
         product_y(0)
         nc.scalar.copy(y_sb[0][:], y_ps[0][:])
-        fetch_pairs(0)
-        combine_pairs(0)
-        put_pairs(0)
-        deal(0)
-        cast_01(nc.vector.tensor_copy, 0, 1, w_hi[0])
-        quantize_w(0, 1)
-        cast_01(nc.vector.tensor_copy, 1, 1, w_hi[1])
-        quantize_w(1, 1)
+        for i in range(2):
+            cast(nc.vector.tensor_copy, hi01[i][:], w_hi[i], 0, whole)
+            quantize_w(i, 1, hi01[i][:].rearrange("p e m j -> p (e m j)"))
+        fetch_pairs(0, pair_tile("pa", 0, "pa0")[:], pair_tile("pb", 0, "pb0")[:])
+        for i in range(2):
+            cast(nc.scalar.copy, all23[i][:, :, HALF:P, :], w_hi[i], 2, whole)
+        put_larger(0, "hi01_1")
         product_y(1)
         nc.vector.tensor_copy(y_sb[1][:], y_ps[1][:])
-        fetch_pairs(1)
-        combine_pairs(1)
-        put_pairs(1)
-        deal(1)
-        for i in range(2):
-            cast_23(nc.vector.tensor_copy, i, 1, w_hi[i])
-            quantize_w(i, 2)
+        fetch_pairs(1, pair_tile("pa", 1, "pa1")[:], pair_tile("pb", 1, "pb1")[:])
+        put_difference(0, "ws1_1")
+        deal(0)
+        put_larger(1, "ra1")
+        late_codes = keep.tile([P, 2, 2, P], U32, name="late_codes", tag="wc1_1", align_bytes=64)
+        for e in range(2):
+            for i in range(2):
+                w_codes[i, 2 + e] = late_codes[:, i, e, :]
+                quantize_w(i, 2 + e, all23[i][:, e, :, :].rearrange("p m j -> p (m j)"))
         for t in (2, 3):
             product_y(t)
             nc.vector.tensor_copy(y_sb[t][:], y_ps[t][:])
-        cand_bytes = gather_packed(xs, cand_t, 0, C, U8, "cand_bytes", "pa1")
-        cand_scales = keep.tile([P, C], U8, name="cand_scales", align_bytes=64)
-        nc.vector.memset(cand_scales[:].bitcast(I32), 0)
-        for r, first in ((0, 0), (1, 1), (2, 16), (3, 17)):
-            nc.sync.dma_start(cand_scales[r:P:32, :].bitcast(I32), cand_bytes[first:P:32, :].bitcast(I32))
-        for t in (2, 3):
-            fetch_pairs(t)
-            combine_pairs(t)
-        cand_words = [gather_packed(xw, cand_t, S * h, S, U32, "cand_words%d" % h, "y_sb%d" % (2 + h)) for h in range(2)]
-        put_pairs(2)
-        put_pairs(3)
-        weigh(dealt[0], 0)
-        weigh(dealt[1], 1)
-        weigh(ub[2], 2)
-        weigh(ub[3], 3)
+        fetch_pairs(2, pair_tile("pa", 2, "pa2")[:], pair_tile("pb", 2, "pb2")[:])
+        put_difference(1, "ws1_2")
+        deal(1)
+        fetch_pairs(3, pair_tile("pa", 3, "pa1")[:], pair_tile("pb", 3, "pb1")[:])
+        put_larger(2, "ra2")
+        put_larger(3, "ra3")
+        put_difference(2, "ra2")
+        put_difference(3, "ub1")
+        cand_scales = [candidate_scales(0, "ws1_3")]
+        cand_words = [gather_packed(xw, cand_t, 0, U32, "cand_words0", "y_sb3")]
+        halves = [slice(0, W), slice(W, S)]
+        z_bf = keep.tile([P, S, PACK], BF16, name="z_bf", tag="pa1", align_bytes=64)
+        weigh(dealt[0], 0, slice(0, S))
+        weigh(dealt[1], 1, slice(0, S))
+        weigh(ub[2], 2, slice(0, S))
+        for cols in halves:
+            weigh(ub[3], 3, cols)
 
         z_codes = keep.tile([P, S], U32, name="z_codes", align_bytes=64)
         z_scales = keep.tile([P, S], U8, name="z_scales", align_bytes=64)
-        nc.vector.quantize_mx(
-            out=z_codes[:].bitcast(FP8X4), scales=z_scales[:], in_=z_bf[:].rearrange("p s t -> p (s t)")
-        )
+        for cols in halves:
+            nc.vector.quantize_mx(
+                out=z_codes[:, cols].bitcast(FP8X4),
+                scales=z_scales[:, cols],
+                in_=z_bf[:, cols, :].rearrange("p s t -> p (s t)"),
+            )
 
         blocks = C // P
-        s_ps = [psum.tile([P, S], F32, name="s_ps%d" % b) for b in range(blocks)]
-        s_sb = [keep.tile([P, S], F32, name="s_sb%d" % b) for b in range(blocks)]
-        s_n7 = [keep.tile([P, S], F32, name="s_n7_%d" % b) for b in range(blocks)]
+        s_ps = {b: psum.tile([P, S], F32, name="s_ps%d" % b) for b in range(1, blocks)}
+        s_sb = [keep.tile([P, S], F32, name="s_sb%d" % b, align_bytes=64) for b in range(blocks)]
+        s_n7 = [keep.tile([P, S], F32, name="s_n7_%d" % b, align_bytes=64) for b in range(blocks)]
         st = [keep.tile([P, S], F32, name="st%d" % b) for b in range(blocks)]
         st_n8 = [keep.tile([P, S], F32, name="st_n8_%d" % b) for b in range(blocks)]
         up = [keep.tile([P, S], F32, name="up%d" % b) for b in range(blocks)]
@@ -229,32 +225,49 @@ def tile_picked_dttzkcpmxpagew_none_p_kernel(
                     dst[:, c0 : c0 + W], window[:].indirect(lst[:, c0 // PER_COL : (c0 + W) // PER_COL]), COPY
                 )
 
-        for b in range(blocks):
-            cols = slice(P * b, P * (b + 1))
+        def scores(dst, b, cols):
+            rows = slice(P * (b % 2), P * (b % 2 + 1))
             nc.tensor.matmul_mx(
-                out=s_ps[b][:],
-                lhsT=cand_words[b // 2][:, P * (b % 2) : P * (b % 2 + 1)].bitcast(FP8X4),
-                lhsT_scale=cand_scales[:, cols],
-                rhs=z_codes[:].bitcast(FP8X4),
-                rhs_scale=z_scales[:],
+                out=dst,
+                lhsT=cand_words[b // 2][:, rows].bitcast(FP8X4),
+                lhsT_scale=cand_scales[b // 2][:, rows],
+                rhs=z_codes[:, cols].bitcast(FP8X4),
+                rhs_scale=z_scales[:, cols],
                 start=True,
                 stop=True,
             )
-            if b == 0:
-                nc.scalar.activation(s_sb[b][:], s_ps[b][:], COPY, scale=SCORE_SCALE)
-            else:
-                nc.vector.tensor_scalar(s_sb[b][:], s_ps[b][:], SCORE_SCALE, None, MULT)
+
+        for h, cols in enumerate(halves):
+            first_ps = psum.tile([P, W], F32, name="first_ps%d" % h, tag="y_ps%d" % h)
+            scores(first_ps[:], 0, cols)
+            nc.scalar.activation(s_sb[0][:, cols], first_ps[:], COPY, scale=SCORE_SCALE)
+        def plain_scores(b):
+            scores(s_ps[b][:], b, slice(0, S))
+            nc.vector.tensor_scalar(s_sb[b][:], s_ps[b][:], SCORE_SCALE, None, MULT)
 
         def first_step(b):
             fetch_halves(s_n7[b], s_sb[b], n7_t)
             nc.vector.tensor_tensor(st[b][:], s_sb[b][:], s_n7[b][:], SUB)
 
-        first_step(0)
-        for b in range(blocks):
-            if b + 1 < blocks:
-                first_step(b + 1)
+        def second_step(b):
             fetch_halves(st_n8[b], st[b], n8_t)
             nc.vector.tensor_tensor(up[b][:], st[b][:], st_n8[b][:], MAX)
             nc.scalar.activation(page[b][:].indirect(n5_t[:]), st[b][:], COPY)
+
+        def finish(b):
             nc.scalar.activation(page[b][:].indirect(n6_t[:]), up[b][:], COPY)
             nc.sync.dma_start(out[P * b : P * (b + 1), :], page[b][:])
+
+        plain_scores(1)
+        first_step(0)
+        cand_scales.append(candidate_scales(1, "s_sb0"))
+        cand_words.append(gather_packed(xw, cand_t, S, U32, "cand_words1", "s_n7_0"))
+        plain_scores(2)
+        plain_scores(3)
+        for b in range(blocks):
+            if b + 1 < blocks:
+                first_step(b + 1)
+            second_step(b)
+            if b > 0:
+                finish(b - 1)
+        finish(blocks - 1)

@@ -73,21 +73,16 @@ def tile_picked_dttzkcpmxpagew_none_p_kernel(
         n5_t = load_list(n5, "n5_t")
         n6_t = load_list(n6, "n6_t")
 
-        def gather_packed(window, lst, first, dtype, name, tag):
+        def gather_packed(got, window, lst, first):
+            nc.vector.tensor_copy(got, window[:].indirect(lst[:, first // PER_COL : (first + S) // PER_COL]))
+
+        def gathered(window, lst, first, dtype, name, tag):
             got = keep.tile([P, S], dtype, name=name, tag=tag, align_bytes=64)
-            nc.vector.tensor_copy(got[:], window[:].indirect(lst[:, first // PER_COL : (first + S) // PER_COL]))
+            gather_packed(got[:], window, lst, first)
             return got
 
-        def candidate_scales(h, tag):
-            picked = gather_packed(xs, cand_t, S * h, U8, "cand_bytes%d" % h, tag)
-            placed = keep.tile([P, S], U8, name="cand_scales%d" % h, align_bytes=64)
-            nc.vector.tensor_copy(placed[:].bitcast(I32), picked[:].bitcast(I32))
-            for r in (2, 3):
-                nc.sync.dma_start(placed[r:P:32, :].bitcast(I32), picked[14 + r : P : 32, :].bitcast(I32))
-            return placed
-
-        tok_scales = [gather_packed(xs, offs_t, 0, U8, "offs_s", "offs_s"), gather_packed(xs, two_t, 0, U8, "two_s", "two_s")]
-        tok_words = [gather_packed(xw, offs_t, 0, U32, "offs_w", "offs_w"), gather_packed(xw, two_t, 0, U32, "two_w", "two_w")]
+        tok_scales = [gathered(xs, offs_t, 0, U8, "offs_s", "offs_s"), gathered(xs, two_t, 0, U8, "two_s", "two_s")]
+        tok_words = [gathered(xw, offs_t, 0, U32, "offs_w", "offs_w"), gathered(xw, two_t, 0, U32, "two_w", "two_w")]
 
         w_scales = {
             (i, t): keep.tile([P, P], U8, name="ws%d_%d" % (i, t), align_bytes=64) for i in range(2) for t in range(PACK)
@@ -166,20 +161,20 @@ def tile_picked_dttzkcpmxpagew_none_p_kernel(
             cast(nc.vector.tensor_copy, hi01[i][:], w_hi[i], 0, whole)
             quantize_w(i, 1, hi01[i][:].rearrange("p e m j -> p (e m j)"))
         fetch_pairs(0, pair_tile("pa", 0, "pa0")[:], pair_tile("pb", 0, "pb0")[:])
-        for i in range(2):
-            cast(nc.scalar.copy, all23[i][:, :, HALF:P, :], w_hi[i], 2, whole)
+        cast(nc.vector.tensor_copy, all23[0][:, :, HALF:P, :], w_hi[0], 2, whole)
+        cast(nc.scalar.copy, all23[1][:, :, HALF:P, :], w_hi[1], 2, whole)
         put_larger(0, "hi01_1")
         product_y(1)
         nc.vector.tensor_copy(y_sb[1][:], y_ps[1][:])
         fetch_pairs(1, pair_tile("pa", 1, "pa1")[:], pair_tile("pb", 1, "pb1")[:])
         put_difference(0, "ws1_1")
         deal(0)
-        put_larger(1, "ra1")
         late_codes = keep.tile([P, 2, 2, P], U32, name="late_codes", tag="wc1_1", align_bytes=64)
         for e in range(2):
             for i in range(2):
                 w_codes[i, 2 + e] = late_codes[:, i, e, :]
                 quantize_w(i, 2 + e, all23[i][:, e, :, :].rearrange("p m j -> p (m j)"))
+        put_larger(1, "ra1")
         for t in (2, 3):
             product_y(t)
             nc.vector.tensor_copy(y_sb[t][:], y_ps[t][:])
@@ -191,8 +186,14 @@ def tile_picked_dttzkcpmxpagew_none_p_kernel(
         put_larger(3, "ra3")
         put_difference(2, "ra2")
         put_difference(3, "ub1")
-        cand_scales = [candidate_scales(0, "ws1_3")]
-        cand_words = [gather_packed(xw, cand_t, 0, U32, "cand_words0", "y_sb3")]
+        cand_bytes = keep.tile([P, C], U8, name="cand_bytes", tag="ws1_3", align_bytes=64)
+        for first in range(0, C, S):
+            gather_packed(cand_bytes[:, first : first + S], xs, cand_t, first)
+        cand_scales = keep.tile([P, C], U8, name="cand_scales", align_bytes=64)
+        nc.vector.tensor_copy(cand_scales[:].bitcast(I32), cand_bytes[:].bitcast(I32))
+        for r in (2, 3):
+            nc.sync.dma_start(cand_scales[r:P:32, :].bitcast(I32), cand_bytes[14 + r : P : 32, :].bitcast(I32))
+        cand_words = [gathered(xw, cand_t, S * h, U32, "cand_words%d" % h, "y_sb%d" % (2 + h)) for h in range(2)]
         halves = [slice(0, W), slice(W, S)]
         z_bf = keep.tile([P, S, PACK], BF16, name="z_bf", tag="pa1", align_bytes=64)
         weigh(dealt[0], 0, slice(0, S))
@@ -212,25 +213,19 @@ def tile_picked_dttzkcpmxpagew_none_p_kernel(
 
         blocks = C // P
         s_ps = {b: psum.tile([P, S], F32, name="s_ps%d" % b) for b in range(1, blocks)}
-        s_sb = [keep.tile([P, S], F32, name="s_sb%d" % b, align_bytes=64) for b in range(blocks)]
+        s_sb = [keep.tile([P, S + PER_COL], F32, name="s_sb%d" % b, align_bytes=64) for b in range(blocks)]
         s_n7 = [keep.tile([P, S], F32, name="s_n7_%d" % b, align_bytes=64) for b in range(blocks)]
-        st = [keep.tile([P, S], F32, name="st%d" % b) for b in range(blocks)]
+        st = [keep.tile([P, S + PER_COL], F32, name="st%d" % b) for b in range(blocks)]
         st_n8 = [keep.tile([P, S], F32, name="st_n8_%d" % b) for b in range(blocks)]
         up = [keep.tile([P, S], F32, name="up%d" % b) for b in range(blocks)]
         page = [keep.tile([P, U], F32, name="page%d" % b) for b in range(blocks)]
-
-        def fetch_halves(dst, window, lst):
-            for c0 in range(0, S, W):
-                nc.scalar.activation(
-                    dst[:, c0 : c0 + W], window[:].indirect(lst[:, c0 // PER_COL : (c0 + W) // PER_COL]), COPY
-                )
 
         def scores(dst, b, cols):
             rows = slice(P * (b % 2), P * (b % 2 + 1))
             nc.tensor.matmul_mx(
                 out=dst,
                 lhsT=cand_words[b // 2][:, rows].bitcast(FP8X4),
-                lhsT_scale=cand_scales[b // 2][:, rows],
+                lhsT_scale=cand_scales[:, P * b : P * (b + 1)],
                 rhs=z_codes[:, cols].bitcast(FP8X4),
                 rhs_scale=z_scales[:, cols],
                 start=True,
@@ -243,27 +238,24 @@ def tile_picked_dttzkcpmxpagew_none_p_kernel(
             nc.scalar.activation(s_sb[0][:, cols], first_ps[:], COPY, scale=SCORE_SCALE)
         def plain_scores(b):
             scores(s_ps[b][:], b, slice(0, S))
-            nc.vector.tensor_scalar(s_sb[b][:], s_ps[b][:], SCORE_SCALE, None, MULT)
+            nc.vector.tensor_scalar(s_sb[b][:, 0:S], s_ps[b][:], SCORE_SCALE, None, MULT)
 
         def first_step(b):
-            fetch_halves(s_n7[b], s_sb[b], n7_t)
-            nc.vector.tensor_tensor(st[b][:], s_sb[b][:], s_n7[b][:], SUB)
+            nc.scalar.activation(s_n7[b][:], s_sb[b][:].indirect(n7_t[:]), COPY)
+            nc.vector.tensor_tensor(st[b][:, 0:S], s_sb[b][:, 0:S], s_n7[b][:], SUB)
 
         def second_step(b):
-            fetch_halves(st_n8[b], st[b], n8_t)
-            nc.vector.tensor_tensor(up[b][:], st[b][:], st_n8[b][:], MAX)
-            nc.scalar.activation(page[b][:].indirect(n5_t[:]), st[b][:], COPY)
+            nc.scalar.activation(st_n8[b][:], st[b][:].indirect(n8_t[:]), COPY)
+            nc.vector.tensor_tensor(up[b][:], st[b][:, 0:S], st_n8[b][:], MAX)
+            nc.scalar.activation(page[b][:].indirect(n5_t[:]), st[b][:, 0:S], COPY)
 
         def finish(b):
             nc.scalar.activation(page[b][:].indirect(n6_t[:]), up[b][:], COPY)
             nc.sync.dma_start(out[P * b : P * (b + 1), :], page[b][:])
 
-        plain_scores(1)
+        for b in range(1, blocks):
+            plain_scores(b)
         first_step(0)
-        cand_scales.append(candidate_scales(1, "s_sb0"))
-        cand_words.append(gather_packed(xw, cand_t, S, U32, "cand_words1", "s_n7_0"))
-        plain_scores(2)
-        plain_scores(3)
         for b in range(blocks):
             if b + 1 < blocks:
                 first_step(b + 1)

@@ -49,8 +49,8 @@ def tile_picked_dttzkcpmxpagew_none_p_kernel(
 
         xs = keep.tile([P, T], U8, name="xs", align_bytes=64)
         nc.vector.memset(xs[:].bitcast(I32), 0)
-        offs_t = load_list(offs, "offs_t")
         w_lo = [load_w(w1, 0, "w1_lo")]
+        offs_t = load_list(offs, "offs_t")
         two_t = load_list(two, "two_t")
         for r, part_step in ((0, 16), (1, 16), (2, 32), (3, 32)):
             nc.sync.dma_start(
@@ -100,20 +100,20 @@ def tile_picked_dttzkcpmxpagew_none_p_kernel(
         def quantize_w(i, t, staged):
             nc.vector.quantize_mx(out=w_codes[i, t].bitcast(FP8X4), scales=w_scales[i, t][:], in_=staged)
 
-        y_ps = [psum.tile([P, S], F32, name="y_ps%d" % t) for t in range(PACK)]
+        y_ps = {t: psum.tile([P, S], F32, name="y_ps%d" % t) for t in (2, 3)}
         y_sb = [keep.tile([P, S], F32, name="y_sb%d" % t, align_bytes=64) for t in range(PACK)]
         pa, pb, ra = {}, {}, {}
         ub = [keep.tile([P, S], F32, name="ub%d" % t, align_bytes=64) for t in range(PACK)]
         dealt = [keep.tile([P, S], F32, name="dealt%d" % e, align_bytes=64) for e in range(2)]
 
-        def product_y(t):
+        def product_y(t, dst, cols):
             for i in range(2):
                 nc.tensor.matmul_mx(
-                    out=y_ps[t][:],
+                    out=dst,
                     lhsT=w_codes[i, t].bitcast(FP8X4),
                     lhsT_scale=w_scales[i, t][:],
-                    rhs=tok_words[i][:].bitcast(FP8X4),
-                    rhs_scale=tok_scales[i][:],
+                    rhs=tok_words[i][:, cols].bitcast(FP8X4),
+                    rhs_scale=tok_scales[i][:, cols],
                     start=(i == 0),
                     stop=(i == 1),
                 )
@@ -155,8 +155,15 @@ def tile_picked_dttzkcpmxpagew_none_p_kernel(
         cast(nc.scalar.copy, lo01[1][:], w_lo[1], 0, slice(quarter, HALF))
         quantize_w(1, 0, lo01[1][:].rearrange("p e m j -> p (e m j)"))
         cast(nc.scalar.copy, all23[1][:, :, 0:HALF, :], w_lo[1], 2, whole)
-        product_y(0)
-        nc.scalar.copy(y_sb[0][:], y_ps[0][:])
+        halves = [slice(0, W), slice(W, S)]
+
+        def product_y_by_halves(t, copy):
+            for h, cols in enumerate(halves):
+                half_ps = psum.tile([P, W], F32, name="y%d_ps%d" % (t, h), tag="half_ps%d" % (2 * t + h))
+                product_y(t, half_ps[:], cols)
+                copy(y_sb[t][:, cols], half_ps[:])
+
+        product_y_by_halves(0, nc.scalar.copy)
         for i in range(2):
             cast(nc.vector.tensor_copy, hi01[i][:], w_hi[i], 0, whole)
             quantize_w(i, 1, hi01[i][:].rearrange("p e m j -> p (e m j)"))
@@ -164,8 +171,7 @@ def tile_picked_dttzkcpmxpagew_none_p_kernel(
         cast(nc.vector.tensor_copy, all23[0][:, :, HALF:P, :], w_hi[0], 2, whole)
         cast(nc.scalar.copy, all23[1][:, :, HALF:P, :], w_hi[1], 2, whole)
         put_larger(0, "hi01_1")
-        product_y(1)
-        nc.vector.tensor_copy(y_sb[1][:], y_ps[1][:])
+        product_y_by_halves(1, nc.vector.tensor_copy)
         fetch_pairs(1, pair_tile("pa", 1, "pa1")[:], pair_tile("pb", 1, "pb1")[:])
         put_difference(0, "ws1_1")
         deal(0)
@@ -176,7 +182,7 @@ def tile_picked_dttzkcpmxpagew_none_p_kernel(
                 quantize_w(i, 2 + e, all23[i][:, e, :, :].rearrange("p m j -> p (m j)"))
         put_larger(1, "ra1")
         for t in (2, 3):
-            product_y(t)
+            product_y(t, y_ps[t][:], slice(0, S))
             nc.vector.tensor_copy(y_sb[t][:], y_ps[t][:])
         fetch_pairs(2, pair_tile("pa", 2, "pa2")[:], pair_tile("pb", 2, "pb2")[:])
         put_difference(1, "ws1_2")
@@ -194,7 +200,6 @@ def tile_picked_dttzkcpmxpagew_none_p_kernel(
         for r in (2, 3):
             nc.sync.dma_start(cand_scales[r:P:32, :].bitcast(I32), cand_bytes[14 + r : P : 32, :].bitcast(I32))
         cand_words = [gathered(xw, cand_t, S * h, U32, "cand_words%d" % h, "y_sb%d" % (2 + h)) for h in range(2)]
-        halves = [slice(0, W), slice(W, S)]
         z_bf = keep.tile([P, S, PACK], BF16, name="z_bf", tag="pa1", align_bytes=64)
         weigh(dealt[0], 0, slice(0, S))
         weigh(dealt[1], 1, slice(0, S))
@@ -212,7 +217,7 @@ def tile_picked_dttzkcpmxpagew_none_p_kernel(
             )
 
         blocks = C // P
-        s_ps = {b: psum.tile([P, S], F32, name="s_ps%d" % b) for b in range(1, blocks)}
+        s_ps = {b: psum.tile([P, S], F32, name="s_ps%d" % b, tag=tag) for b, tag in ((1, "half_ps2"), (2, "half_ps3"), (3, "s_ps3"))}
         s_sb = [keep.tile([P, S + PER_COL], F32, name="s_sb%d" % b, align_bytes=64) for b in range(blocks)]
         s_n7 = [keep.tile([P, S], F32, name="s_n7_%d" % b, align_bytes=64) for b in range(blocks)]
         st = [keep.tile([P, S + PER_COL], F32, name="st%d" % b) for b in range(blocks)]
@@ -233,7 +238,7 @@ def tile_picked_dttzkcpmxpagew_none_p_kernel(
             )
 
         for h, cols in enumerate(halves):
-            first_ps = psum.tile([P, W], F32, name="first_ps%d" % h, tag="y_ps%d" % h)
+            first_ps = psum.tile([P, W], F32, name="first_ps%d" % h, tag="half_ps%d" % h)
             scores(first_ps[:], 0, cols)
             nc.scalar.activation(s_sb[0][:, cols], first_ps[:], COPY, scale=SCORE_SCALE)
         def plain_scores(b):

from contextlib import ExitStack

import concourse.mybir as mybir

F32 = mybir.dt.float32
BF16 = mybir.dt.bfloat16
I32 = mybir.dt.int32
U32 = mybir.dt.uint32
U16 = mybir.dt.uint16
U8 = mybir.dt.uint8
FP8X4 = mybir.dt.float8_e4m3fn_x4
COPY = mybir.ActivationFunctionType.Copy
MULT = mybir.AluOpType.mult
MAX = mybir.AluOpType.max
SUB = mybir.AluOpType.subtract

P = 128
HALF = 64
PACK = 4
T = 2048
S = 256
W = 128
C = 512
U = 512
PER_COL = 16
SCORE_SCALE = 0.0625

FLOPS = 402653184


def tile_picked_dttzkcpmxpagew_none_p_kernel(
    tc, x_words, x_scales, w1, w2, gs, offs, two, n1, n2, n3, n4, cand, n5, n6, n7, n8, out
):
    nc = tc.nc
    with ExitStack() as ctx:
        keep = ctx.enter_context(tc.tile_pool(name="keep", bufs=1))
        psum = ctx.enter_context(tc.psum_pool(name="psum", bufs=1))

        def load_list(src, name):
            lst = keep.tile(list(src.shape), U16, name=name)
            nc.sync.dma_start(lst[:], src)
            return lst

        def load_w(w, half, name):
            raw = keep.tile([P, PACK, 2 * P], F32, name=name)
            cols = slice(2 * P * half, 2 * P * (half + 1))
            nc.sync.dma_start(raw[:], w.rearrange("(p j) c -> p j c", j=PACK)[:, :, cols])
            return raw

        xs = keep.tile([P, T], U8, name="xs", align_bytes=64)
        nc.vector.memset(xs[:].bitcast(I32), 0)
        w_lo = [load_w(w1, 0, "w1_lo")]
        offs_t = load_list(offs, "offs_t")
        two_t = load_list(two, "two_t")
        for r, part_step in ((0, 16), (1, 16), (2, 32), (3, 32)):
            nc.sync.dma_start(
                xs[r:P:part_step, :].bitcast(I32), x_scales[0, r : 16 : part_step // 8, :].bitcast(I32)
            )
        xw = keep.tile([P, T], U32, name="xw", align_bytes=64)
        nc.sync.dma_start(xw[:].bitcast(I32), x_words[0].rearrange("p n t -> p (n t)").bitcast(I32))
        w_lo.append(load_w(w2, 0, "w2_lo"))
        n1_t = load_list(n1, "n1_t")
        n2_t = load_list(n2, "n2_t")
        w_hi = [load_w(w1, 1, "w1_hi")]
        n3_t = load_list(n3, "n3_t")
        n4_t = load_list(n4, "n4_t")
        w_hi.append(load_w(w2, 1, "w2_hi"))
        cand_t = load_list(cand, "cand_t")
        gs_t = keep.tile([P, PACK], F32, name="gs_t")
        nc.sync.dma_start(gs_t[:], gs.rearrange("(p t) o -> p (t o)", t=PACK))
        n7_t = load_list(n7, "n7_t")
        n8_t = load_list(n8, "n8_t")
        n5_t = load_list(n5, "n5_t")
        n6_t = load_list(n6, "n6_t")

        def gather_packed(got, window, lst, first):
            nc.vector.tensor_copy(got, window[:].indirect(lst[:, first // PER_COL : (first + S) // PER_COL]))

        def gathered(window, lst, first, dtype, name, tag):
            got = keep.tile([P, S], dtype, name=name, tag=tag, align_bytes=64)
            gather_packed(got[:], window, lst, first)
            return got

        tok_scales = [gathered(xs, offs_t, 0, U8, "offs_s", "offs_s"), gathered(xs, two_t, 0, U8, "two_s", "two_s")]
        tok_words = [gathered(xw, offs_t, 0, U32, "offs_w", "offs_w"), gathered(xw, two_t, 0, U32, "two_w", "two_w")]

        w_scales = {
            (i, t): keep.tile([P, P], U8, name="ws%d_%d" % (i, t), align_bytes=64) for i in range(2) for t in range(PACK)
        }
        w_codes = {
            (i, t): keep.tile([P, P], U32, name="wc%d_%d" % (i, t), align_bytes=64)[:]
            for i in range(2)
            for t in range(2)
        }

        def cast(copy, dst, raw, first_class, ms):
            src = raw[:].rearrange("p j (m e) -> p m e j", e=PACK)
            copy(dst.rearrange("p e m j -> p m e j")[:, ms, :, :], src[:, ms, first_class : first_class + 2, :])

        def quantize_w(i, t, staged):
            nc.vector.quantize_mx(out=w_codes[i, t].bitcast(FP8X4), scales=w_scales[i, t][:], in_=staged)

        y_ps = {t: psum.tile([P, S], F32, name="y_ps%d" % t) for t in (2, 3)}
        y_sb = [keep.tile([P, S], F32, name="y_sb%d" % t, align_bytes=64) for t in range(PACK)]
        pa, pb, ra = {}, {}, {}
        ub = [keep.tile([P, S], F32, name="ub%d" % t, align_bytes=64) for t in range(PACK)]
        dealt = [keep.tile([P, S], F32, name="dealt%d" % e, align_bytes=64) for e in range(2)]

        def product_y(t, dst, cols):
            for i in range(2):
                nc.tensor.matmul_mx(
                    out=dst,
                    lhsT=w_codes[i, t].bitcast(FP8X4),
                    lhsT_scale=w_scales[i, t][:],
                    rhs=tok_words[i][:, cols].bitcast(FP8X4),
                    rhs_scale=tok_scales[i][:, cols],
                    start=(i == 0),
                    stop=(i == 1),
                )

        def pair_tile(name, t, tag):
            return keep.tile([P, W], F32, name="%s%d" % (name, t), tag=tag, align_bytes=64)

        def fetch_pairs(t, dst_a, dst_b):
            pa[t], pb[t] = dst_a, dst_b
            nc.scalar.activation(pa[t], y_sb[t][:].indirect(n1_t[:]), COPY)
            nc.scalar.activation(pb[t], y_sb[t][:].indirect(n2_t[:]), COPY)

        def put_larger(t, tag):
            ra[t] = pair_tile("ra", t, tag)
            nc.vector.tensor_tensor(ra[t][:], pa[t], pb[t], MAX)
            nc.scalar.activation(ub[t][:].indirect(n3_t[:]), ra[t][:], COPY)

        def put_difference(t, tag):
            rb = pair_tile("rb", t, tag)
            nc.vector.tensor_tensor(rb[:], pa[t], pb[t], SUB)
            nc.scalar.activation(ub[t][:].indirect(n4_t[:]), rb[:], COPY)

        def deal(t):
            for e in range(2):
                nc.sync.dma_start(dealt[e][HALF * t : HALF * (t + 1), :], ub[t][HALF * e : HALF * (e + 1), :])

        def weigh(src, e, cols):
            nc.vector.tensor_scalar(z_bf[:, cols, e], src[:, cols], gs_t[:, e : e + 1], None, MULT)

        quarter = HALF // 2
        whole = slice(0, HALF)
        lo01 = [keep.tile([P, 2, HALF, PACK], BF16, name="lo01_%d" % i, align_bytes=64) for i in range(2)]
        hi01 = [keep.tile([P, 2, HALF, PACK], BF16, name="hi01_%d" % i, align_bytes=64) for i in range(2)]
        all23 = [keep.tile([P, 2, P, PACK], BF16, name="all23_%d" % i, align_bytes=64) for i in range(2)]
        cast(nc.scalar.copy, lo01[0][:], w_lo[0], 0, whole)
        cast(nc.scalar.copy, all23[0][:, :, 0:HALF, :], w_lo[0], 2, whole)
        quantize_w(0, 0, lo01[0][:].rearrange("p e m j -> p (e m j)"))
        cast(nc.vector.tensor_copy, lo01[1][:], w_lo[1], 0, slice(0, quarter))
        cast(nc.scalar.copy, lo01[1][:], w_lo[1], 0, slice(quarter, HALF))
        quantize_w(1, 0, lo01[1][:].rearrange("p e m j -> p (e m j)"))
        cast(nc.scalar.copy, all23[1][:, :, 0:HALF, :], w_lo[1], 2, whole)
        halves = [slice(0, W), slice(W, S)]

        def product_y_by_halves(t, copy):
            for h, cols in enumerate(halves):
                half_ps = psum.tile([P, W], F32, name="y%d_ps%d" % (t, h), tag="half_ps%d" % (2 * t + h))
                product_y(t, half_ps[:], cols)
                copy(y_sb[t][:, cols], half_ps[:])

        product_y_by_halves(0, nc.scalar.copy)
        for i in range(2):
            cast(nc.vector.tensor_copy, hi01[i][:], w_hi[i], 0, whole)
            quantize_w(i, 1, hi01[i][:].rearrange("p e m j -> p (e m j)"))
        fetch_pairs(0, pair_tile("pa", 0, "pa0")[:], pair_tile("pb", 0, "pb0")[:])
        cast(nc.vector.tensor_copy, all23[0][:, :, HALF:P, :], w_hi[0], 2, whole)
        cast(nc.scalar.copy, all23[1][:, :, HALF:P, :], w_hi[1], 2, whole)
        put_larger(0, "hi01_1")
        product_y_by_halves(1, nc.vector.tensor_copy)
        fetch_pairs(1, pair_tile("pa", 1, "pa1")[:], pair_tile("pb", 1, "pb1")[:])
        put_difference(0, "ws1_1")
        deal(0)
        late_codes = keep.tile([P, 2, 2, P], U32, name="late_codes", tag="wc1_1", align_bytes=64)
        for e in range(2):
            for i in range(2):
                w_codes[i, 2 + e] = late_codes[:, i, e, :]
                quantize_w(i, 2 + e, all23[i][:, e, :, :].rearrange("p m j -> p (m j)"))
        put_larger(1, "ra1")
        for t in (2, 3):
            product_y(t, y_ps[t][:], slice(0, S))
            nc.vector.tensor_copy(y_sb[t][:], y_ps[t][:])
        fetch_pairs(2, pair_tile("pa", 2, "pa2")[:], pair_tile("pb", 2, "pb2")[:])
        put_difference(1, "ws1_2")
        deal(1)
        fetch_pairs(3, pair_tile("pa", 3, "pa1")[:], pair_tile("pb", 3, "pb1")[:])
        put_larger(2, "ra2")
        put_larger(3, "ra3")
        put_difference(2, "ra2")
        put_difference(3, "ub1")
        cand_bytes = keep.tile([P, C], U8, name="cand_bytes", tag="ws1_3", align_bytes=64)
        for first in range(0, C, S):
            gather_packed(cand_bytes[:, first : first + S], xs, cand_t, first)
        cand_scales = keep.tile([P, C], U8, name="cand_scales", align_bytes=64)
        nc.vector.tensor_copy(cand_scales[:].bitcast(I32), cand_bytes[:].bitcast(I32))
        for r in (2, 3):
            nc.sync.dma_start(cand_scales[r:P:32, :].bitcast(I32), cand_bytes[14 + r : P : 32, :].bitcast(I32))
        cand_words = [gathered(xw, cand_t, S * h, U32, "cand_words%d" % h, "y_sb%d" % (2 + h)) for h in range(2)]
        z_bf = keep.tile([P, S, PACK], BF16, name="z_bf", tag="pa1", align_bytes=64)
        weigh(dealt[0], 0, slice(0, S))
        weigh(dealt[1], 1, slice(0, S))
        weigh(ub[2], 2, slice(0, S))
        for cols in halves:
            weigh(ub[3], 3, cols)

        z_codes = keep.tile([P, S], U32, name="z_codes", align_bytes=64)
        z_scales = keep.tile([P, S], U8, name="z_scales", align_bytes=64)
        for cols in halves:
            nc.vector.quantize_mx(
                out=z_codes[:, cols].bitcast(FP8X4),
                scales=z_scales[:, cols],
                in_=z_bf[:, cols, :].rearrange("p s t -> p (s t)"),
            )

        blocks = C // P
        s_ps = {b: psum.tile([P, S], F32, name="s_ps%d" % b, tag=tag) for b, tag in ((1, "half_ps2"), (2, "half_ps3"), (3, "s_ps3"))}
        s_sb = [keep.tile([P, S + PER_COL], F32, name="s_sb%d" % b, align_bytes=64) for b in range(blocks)]
        s_n7 = [keep.tile([P, S], F32, name="s_n7_%d" % b, align_bytes=64) for b in range(blocks)]
        st = [keep.tile([P, S + PER_COL], F32, name="st%d" % b) for b in range(blocks)]
        st_n8 = [keep.tile([P, S], F32, name="st_n8_%d" % b) for b in range(blocks)]
        up = [keep.tile([P, S], F32, name="up%d" % b) for b in range(blocks)]
        page = [keep.tile([P, U], F32, name="page%d" % b) for b in range(blocks)]

        def scores(dst, b, cols):
            rows = slice(P * (b % 2), P * (b % 2 + 1))
            nc.tensor.matmul_mx(
                out=dst,
                lhsT=cand_words[b // 2][:, rows].bitcast(FP8X4),
                lhsT_scale=cand_scales[:, P * b : P * (b + 1)],
                rhs=z_codes[:, cols].bitcast(FP8X4),
                rhs_scale=z_scales[:, cols],
                start=True,
                stop=True,
            )

        for h, cols in enumerate(halves):
            first_ps = psum.tile([P, W], F32, name="first_ps%d" % h, tag="half_ps%d" % h)
            scores(first_ps[:], 0, cols)
            nc.scalar.activation(s_sb[0][:, cols], first_ps[:], COPY, scale=SCORE_SCALE)
        def plain_scores(b):
            scores(s_ps[b][:], b, slice(0, S))
            nc.vector.tensor_scalar(s_sb[b][:, 0:S], s_ps[b][:], SCORE_SCALE, None, MULT)

        def first_step(b):
            nc.scalar.activation(s_n7[b][:], s_sb[b][:].indirect(n7_t[:]), COPY)
            nc.vector.tensor_tensor(st[b][:, 0:S], s_sb[b][:, 0:S], s_n7[b][:], SUB)

        def second_step(b):
            nc.scalar.activation(st_n8[b][:], st[b][:].indirect(n8_t[:]), COPY)
            nc.vector.tensor_tensor(up[b][:], st[b][:, 0:S], st_n8[b][:], MAX)
            nc.scalar.activation(page[b][:].indirect(n5_t[:]), st[b][:, 0:S], COPY)

        def finish(b):
            nc.scalar.activation(page[b][:].indirect(n6_t[:]), up[b][:], COPY)
            nc.sync.dma_start(out[P * b : P * (b + 1), :], page[b][:])

        for b in range(1, blocks):
            plain_scores(b)
        first_step(0)
        for b in range(blocks):
            if b + 1 < blocks:
                first_step(b + 1)
            second_step(b)
            if b > 0:
                finish(b - 1)
        finish(blocks - 1)
